import numpy as np
import ml_dtypes


def mxq(x, axis, fmt="e4m3"):
    dtype, down = {"e4m3": (ml_dtypes.float8_e4m3fn, 7), "e5m2": (ml_dtypes.float8_e5m2, 14)}[fmt]
    v = np.moveaxis(np.asarray(x, np.float32).astype(ml_dtypes.bfloat16).astype(np.float64), axis, -1)
    blocks = v.reshape(v.shape[:-1] + (-1, 32))
    amax = np.abs(blocks).max(-1, keepdims=True)
    byte = np.maximum(np.where(amax > 0, np.frexp(amax)[1] - 1 + 127, 0) - down, 1)
    scale = np.exp2(byte - 127.0)
    codes = (blocks / scale).astype(np.float32).astype(dtype).astype(np.float64)
    return np.moveaxis((codes * scale).reshape(v.shape), -1, axis)


WIDE = False


def mx_kscale(k):
    if not WIDE:
        return np.ones(k)
    levels = np.array([10, -10, 5, -5, 0])
    if k % 512:
        return np.exp2(np.random.permutation(np.resize(levels, k // 32))).repeat(32)
    a = np.empty((k // 512, 16))
    for p in range(k // 512):
        a[p, :8] = np.random.permutation(np.resize(levels, 8))
        for g in range(8):
            far = levels[np.abs(levels - a[p, g]) >= 10]
            a[p, g + 8] = far[np.random.randint(len(far))]
    return np.exp2(a.ravel()).repeat(32)


def f64(x):
    return np.asarray(x).astype(np.float64)


def striped(idx):
    return np.tile(idx.reshape(-1, 16).T, (8, 1)).astype(np.uint16)


def unstriped(offs):
    return offs[:16].T.reshape(-1).astype(np.int64)


def pack_weight(w):
    k, n = w.shape
    w = f64(np.asarray(w, np.float32).astype(ml_dtypes.bfloat16)).reshape(k // 32, 32, n)
    amax = np.abs(w).max(1)
    byte = np.clip(np.where(amax > 0, np.frexp(amax)[1] - 1 + 127 - 7, 1), 1, 254)
    scaled = (w * np.exp2(127.0 - byte)[:, None, :]).reshape(k, n).astype(np.float32)
    words = np.ascontiguousarray(scaled.reshape(k // 512, 128, 4, n).transpose(0, 1, 3, 2)).astype(ml_dtypes.float8_e4m3fn).view(np.uint8)
    return words, np.ascontiguousarray(byte.astype(np.uint8).reshape(k // 512, 16, n))


def unpack_weight(words, scales):
    g, p, n, _ = words.shape
    vals = np.ascontiguousarray(words).view(ml_dtypes.float8_e4m3fn).astype(np.float64) * np.repeat(np.exp2(scales.astype(np.float64) - 127.0), 8, axis=1)[..., None]
    return vals.transpose(0, 1, 3, 2).reshape(g * 512, n)


E2M1 = np.array([0.0, 0.5, 1.0, 1.5, 2.0, 3.0, 4.0, 6.0, -0.0, -0.5, -1.0, -1.5, -2.0, -3.0, -4.0, -6.0])


def pack_fp4(w):
    k, n = w.shape
    w = f64(np.asarray(w, np.float32).astype(ml_dtypes.bfloat16)).reshape(k // 32, 32, n)
    amax = np.abs(w).max(1)
    mant, ex = np.frexp(amax / 6.0)
    byte = np.clip(np.where(amax > 0, np.where(mant > 0.5, ex, ex - 1) + 127, 1), 1, 254)
    scaled = (w * np.exp2(127.0 - byte)[:, None, :]).reshape(k, n).astype(np.float32)
    c = np.ascontiguousarray(scaled.reshape(k // 512, 128, 4, n).transpose(0, 1, 3, 2)).astype(ml_dtypes.float4_e2m1fn).view(np.uint8) & 0xF
    words = (c[..., 0::2] | (c[..., 1::2] << 4)).reshape(k // 512, 128, 2 * n)
    return np.ascontiguousarray(words), np.ascontiguousarray(byte.astype(np.uint8).reshape(k // 512, 16, n))


def unpack_fp4(words, scales):
    g, _, n = scales.shape
    words = np.ascontiguousarray(words).reshape(g, 128, n, 2)
    nib = np.empty((g, 128, n, 4), np.uint8)
    nib[..., 0::2] = words & 0xF
    nib[..., 1::2] = words >> 4
    vals = E2M1[nib] * np.repeat(np.exp2(scales.astype(np.float64) - 127.0), 8, axis=1)[..., None]
    return vals.transpose(0, 1, 3, 2).reshape(g * 512, n)


def sigmoid(v):
    return 1.0 / (1.0 + np.exp(-np.maximum(v, -700.0)))


def silu(v):
    return v / (1.0 + np.exp(-np.maximum(v, -700.0)))


K, T, S, N, H, V = 512, 1024, 512, 128, 512, 256


def setup_inputs():
    n = np.random.standard_normal
    s = mx_kscale(K)[:, None]
    u = mx_kscale(H)
    packed_xT = pack_weight(n((K, T)) * s)
    packed_w1 = pack_fp4(n((K, H)) / np.sqrt(K) / s)
    packed_w2 = pack_fp4(n((K, H)) / np.sqrt(K) / s)
    packed_w3 = pack_fp4(n((H, N)) / np.sqrt(H) / u[:, None])
    return {
        "x_words": packed_xT[0],
        "x_scales": packed_xT[1],
        "w1_words": packed_w1[0],
        "w1_scales": packed_w1[1],
        "w2_words": packed_w2[0],
        "w2_scales": packed_w2[1],
        "ctx2": (n((H, V))).astype(np.float32),
        "unit": (np.random.uniform(0.6, 1.4, (H, 1)) * u[:, None]).astype(np.float32),
        "w3_words": packed_w3[0],
        "w3_scales": packed_w3[1],
        "offs": striped(np.random.permutation(T)[:S]),
        "sel": striped(np.random.permutation(S)[:V]),
        "nxt": striped(np.random.permutation(S)),
    }


def reference(x_words, x_scales, w1_words, w1_scales, w2_words, w2_scales, ctx2, unit, w3_words, w3_scales, offs, sel, nxt):
    xq = unpack_weight(x_words, x_scales)[:, unstriped(offs)]
    yr = unpack_fp4(w2_words, w2_scales).T @ xq
    rs = yr[:, unstriped(sel)]
    rw = sigmoid(rs)
    y = unpack_fp4(w1_words, w1_scales).T @ xq
    xs = y[:, unstriped(sel)]
    upd = rw * (silu(xs + f64(ctx2)))
    merged = y.copy()
    merged[:, unstriped(sel)] = upd
    mn = merged[:, unstriped(nxt)]
    hid = f64(unit) * (merged - mn)
    return unpack_fp4(w3_words, w3_scales).T @ mxq(hid, 0, "e4m3")

@@ -1,0 +1,257 @@
+from contextlib import ExitStack
+
+import concourse.mybir as mybir
+
+FLOPS = 603979776
+
+F32 = mybir.dt.float32
+BF16 = mybir.dt.bfloat16
+I32 = mybir.dt.int32
+U32 = mybir.dt.uint32
+U16 = mybir.dt.uint16
+U8 = mybir.dt.uint8
+FP8X4 = mybir.dt.float8_e4m3fn_x4
+FP4X4 = mybir.dt.float4_e2m1fn_x4
+ACT = mybir.ActivationFunctionType
+ALU = mybir.AluOpType
+
+P = 128
+T, S, V, H, N = 1024, 512, 256, 512, 128
+PACK = 4
+CHUNKS = 4
+CHUNK = S // CHUNKS
+
+
+def load_scale_rows(nc, plane, rows):
+    for q in range(4):
+        nc.sync.dma_start(out=plane[32 * q : 32 * q + 4, :].bitcast(I32), in_=rows[0, 4 * q : 4 * q + 4, :].bitcast(I32))
+
+
+def tile_picked_ymodsk_nxt_p_kernel(
+    tc, x_words, x_scales, w1_words, w1_scales, w2_words, w2_scales, ctx2, unit, w3_words, w3_scales, offs, sel, nxt, out
+):
+    nc = tc.nc
+    with ExitStack() as stack:
+        keep = stack.enter_context(tc.tile_pool(name="keep", bufs=1))
+        ring = stack.enter_context(tc.tile_pool(name="ring", bufs=4))
+        psum = stack.enter_context(tc.psum_pool(name="psum", bufs=3))
+        psum_out = stack.enter_context(tc.psum_pool(name="psum_out", bufs=2))
+
+        offs_t = keep.tile([P, S // 16], U16, name="offs_t")
+        sel_t = keep.tile([P, V // 16], U16, name="sel_t")
+        nxt_t = keep.tile([P, S // 16], U16, name="nxt_t")
+        xw_all = keep.tile([P, T], I32, name="xw_all", align_bytes=64)
+        xs_all = keep.tile([P, T], U8, name="xs_all", align_bytes=64)
+        w_raw = [keep.tile([P, 2 * H], U8, name="w_raw%d" % i, align_bytes=64) for i in range(2)]
+        ws_raw = [keep.tile([P, H], U8, name="ws_raw%d" % i, align_bytes=64) for i in range(2)]
+        w3w = keep.tile([P, 2 * N], U8, name="w3w", align_bytes=64)
+        w3s = keep.tile([P, N], U8, name="w3s", align_bytes=64)
+        ctx_t = keep.tile([P, PACK, V], F32, name="ctx_t")
+        unit_t = keep.tile([P, PACK], F32, name="unit_t")
+
+        nc.gpsimd.memset(xs_all[:].bitcast(I32), 0)
+        for plane in (ws_raw[0], ws_raw[1], w3s):
+            nc.gpsimd.memset(plane[:].bitcast(I32), 0)
+
+        nc.sync.dma_start(offs_t[:], offs)
+        load_scale_rows(nc, xs_all, x_scales)
+        nc.sync.dma_start(out=xw_all[:], in_=x_words[0].rearrange("p n t -> p (n t)").bitcast(I32))
+        nc.sync.dma_start(out=w_raw[0][:].bitcast(I32), in_=w2_words[0].bitcast(I32))
+        nc.sync.dma_start(out=w_raw[1][:].bitcast(I32), in_=w1_words[0].bitcast(I32))
+        load_scale_rows(nc, ws_raw[0], w2_scales)
+        load_scale_rows(nc, ws_raw[1], w1_scales)
+        nc.sync.dma_start(sel_t[:], sel)
+        nc.sync.dma_start(out=ctx_t[:], in_=ctx2.rearrange("(p t) v -> p t v", t=PACK))
+        nc.sync.dma_start(out=unit_t[:], in_=unit.rearrange("(p t) o -> p (t o)", t=PACK))
+        nc.sync.dma_start(nxt_t[:], nxt)
+        nc.sync.dma_start(out=w3w[:].bitcast(I32), in_=w3_words[0].bitcast(I32))
+        load_scale_rows(nc, w3s, w3_scales)
+
+        w_deal = [keep.tile([P, 2 * H], U8, name="w_deal%d" % i, align_bytes=64) for i in range(2)]
+        ws_deal = [keep.tile([P, H], U8, name="ws_deal%d" % i, align_bytes=64) for i in range(2)]
+
+        def deal(i):
+            nc.vector.tensor_copy(
+                out=w_deal[i][:].rearrange("p (t m b) -> p t m b", t=PACK, b=2),
+                in_=w_raw[i][:].rearrange("p (m t b) -> p t m b", t=PACK, b=2),
+            )
+            nc.vector.tensor_copy(
+                out=ws_deal[i][:].rearrange("p (t m) -> p t m", t=PACK),
+                in_=ws_raw[i][:].rearrange("p (m t) -> p t m", t=PACK),
+            )
+
+        xs = keep.tile([P, S], U8, name="xs", align_bytes=64)
+        xw = keep.tile([P, S], U32, name="xw", align_bytes=64)
+        nc.vector.tensor_copy(xs[:], xs_all[:].indirect(offs_t[:]))
+        nc.vector.tensor_copy(xw[:], xw_all[:].bitcast(U32).indirect(offs_t[:]))
+        deal(0)
+        deal(1)
+
+        scaled = keep.tile([P, PACK, S], F32, name="scaled")
+        fetched = [keep.tile([P, PACK, CHUNK], F32, name="fetched%d" % h) for h in range(CHUNKS)]
+
+        def product(i, t, tag):
+            acc = psum.tile([P, S], F32, name=tag)
+            nc.tensor.matmul_mx(
+                out=acc[:],
+                lhsT=w_deal[i][:, 2 * P * t : 2 * P * (t + 1)].bitcast(FP4X4),
+                lhsT_scale=ws_deal[i][:, P * t : P * (t + 1)],
+                rhs=xw[:].bitcast(FP8X4),
+                rhs_scale=xs[:],
+                start=True,
+                stop=True,
+            )
+            return acc
+
+        accs, merged, gate, u, su, rw, g = {}, {}, {}, {}, {}, {}, {}
+        for t in range(PACK):
+            merged[t] = ring.tile([P, S], F32, name="merged")
+            gate[t] = ring.tile([P, S], F32, name="gate")
+            u[t] = ring.tile([P, V], F32, name="u")
+            su[t] = ring.tile([P, V], F32, name="su")
+            rw[t] = ring.tile([P, V], F32, name="rw")
+            g[t] = ring.tile([P, V], F32, name="g")
+
+        def ey(t, eng="s"):
+            acc = product(1, t, "y")
+            if eng == "v":
+                nc.vector.tensor_copy(merged[t][:], acc[:])
+            else:
+                nc.scalar.copy(merged[t][:], acc[:])
+
+        def er(t):
+            acc = product(0, t, "yr")
+            nc.scalar.activation(gate[t][:], acc[:], ACT.Sigmoid)
+
+        def add(t):
+            nc.vector.tensor_tensor(u[t][:], merged[t][:].indirect(sel_t[:]), ctx_t[:, t, :], ALU.add)
+
+        def sg(t):
+            nc.scalar.activation(su[t][:], u[t][:], ACT.Sigmoid)
+
+        def gg(t):
+            nc.scalar.activation(rw[t][:], gate[t][:].indirect(sel_t[:]), ACT.Copy)
+
+        def mul(t):
+            nc.vector.tensor_tensor(g[t][:], u[t][:], su[t][:], ALU.mult)
+
+        def gmul(t):
+            nc.vector.tensor_tensor(g[t][:], gate[t][:].indirect(sel_t[:]), su[t][:], ALU.mult)
+
+        def scat(t, other):
+            nc.vector.tensor_tensor(merged[t][:].indirect(sel_t[:]), g[t][:], other[t][:], ALU.mult)
+
+        def scat_s(t, other):
+            upd = ring.tile([P, V], F32, name="upd")
+            nc.vector.tensor_tensor(upd[:], g[t][:], other[t][:], ALU.mult)
+            nc.scalar.activation(merged[t][:].indirect(sel_t[:]), upd[:], ACT.Copy)
+
+        upds = {}
+
+        def upd(t, other):
+            upds[t] = ring.tile([P, V], F32, name="upd")
+            nc.vector.tensor_tensor(upds[t][:], g[t][:], other[t][:], ALU.mult)
+
+        def put(t):
+            nc.scalar.activation(merged[t][:].indirect(sel_t[:]), upds[t][:], ACT.Copy)
+
+        def scale(t, eng):
+            if eng == "v":
+                nc.vector.tensor_scalar(scaled[:, t, :], merged[t][:], unit_t[:, t : t + 1], None, ALU.mult)
+            else:
+                nc.scalar.activation(scaled[:, t, :], merged[t][:], ACT.Copy, scale=unit_t[:, t : t + 1])
+
+        def fetch(t, h, eng):
+            cols = CHUNK // 16
+            src = scaled[:, t, :].indirect(nxt_t[:, cols * h : cols * (h + 1)])
+            if eng == "v":
+                nc.vector.tensor_copy(fetched[h][:, t, :], src)
+            else:
+                nc.scalar.activation(fetched[h][:, t, :], src, ACT.Copy)
+
+        hid = [ring.tile([P, CHUNK * PACK], BF16, name="hid", align_bytes=64) for h in range(CHUNKS)]
+
+        def diff4(h):
+            nc.vector.tensor_tensor(
+                hid[h][:].rearrange("p (c i t) -> p c t i", i=4, t=PACK),
+                scaled[:, :, CHUNK * h : CHUNK * (h + 1)].rearrange("p t (c i) -> p c t i", i=4),
+                fetched[h][:].rearrange("p t (c i) -> p c t i", i=4),
+                ALU.subtract,
+            )
+
+        def finish(h, eng):
+            hw = ring.tile([P, CHUNK], U32, name="hw", align_bytes=64)
+            hs = ring.tile([P, CHUNK], U8, name="hs", align_bytes=64)
+            nc.vector.quantize_mx(out=hw[:].bitcast(FP8X4), scales=hs[:], in_=hid[h][:])
+            acc = psum_out.tile([P, CHUNK], F32, name="acc")
+            nc.tensor.matmul_mx(
+                out=acc[:],
+                lhsT=w3w[:].bitcast(FP4X4),
+                lhsT_scale=w3s[:],
+                rhs=hw[:].bitcast(FP8X4),
+                rhs_scale=hs[:],
+                start=True,
+                stop=True,
+            )
+            res = ring.tile([P, CHUNK], F32, name="res")
+            if eng == "v":
+                nc.vector.tensor_copy(res[:], acc[:])
+            else:
+                nc.scalar.copy(res[:], acc[:])
+            nc.sync.dma_start(out=out[:, CHUNK * h : CHUNK * (h + 1)], in_=res[:])
+
+        er(0)
+        ey(0,"v")
+        ey(1,"s")
+        ey(2,"s")
+        add(0)
+        add(1)
+        ey(3,"s")
+        sg(0)
+        add(2)
+        sg(1)
+        er(1)
+        gmul(0)
+        add(3)
+        sg(2)
+        er(2)
+        upd(0,u)
+        gmul(1)
+        sg(3)
+        er(3)
+        upd(1,u)
+        gmul(2)
+        upd(2,u)
+        gmul(3)
+        put(0)
+        put(1)
+        scale(0,"v")
+        scat(3,u)
+        put(2)
+        scale(1,"v")
+        scale(3,"v")
+        scale(2,"v")
+        fetch(0,0,"v")
+        fetch(1,0,"s")
+        fetch(3,0,"s")
+        fetch(2,0,"s")
+        fetch(0,1,"v")
+        fetch(1,1,"s")
+        fetch(3,1,"s")
+        fetch(2,1,"s")
+        fetch(0,2,"v")
+        fetch(1,2,"s")
+        fetch(3,2,"s")
+        fetch(2,2,"s")
+        fetch(0,3,"v")
+        fetch(1,3,"s")
+        fetch(3,3,"s")
+        fetch(2,3,"s")
+        diff4(0)
+        diff4(1)
+        finish(0,"s")
+        diff4(2)
+        finish(1,"s")
+        diff4(3)
+        finish(2,"s")
+        finish(3,"s")

@@ -49,17 +49,20 @@ def tile_picked_ymodsk_nxt_p_kernel(
         ctx_t = keep.tile([P, PACK, V], F32, name="ctx_t")
         unit_t = keep.tile([P, PACK], F32, name="unit_t")
 
+        warm = keep.tile([P, 16], F32, name="warm")
+        nc.vector.memset(warm[:, 0:1], 0.0)
+        nc.scalar.activation(warm[:, 8:9], warm[:, 0:1], ACT.Sigmoid)
         nc.gpsimd.memset(xs_all[:].bitcast(I32), 0)
-        for plane in (ws_raw[0], ws_raw[1], w3s):
+        for plane in (ws_raw[1], ws_raw[0], w3s):
             nc.gpsimd.memset(plane[:].bitcast(I32), 0)
 
         nc.sync.dma_start(offs_t[:], offs)
         load_scale_rows(nc, xs_all, x_scales)
-        nc.sync.dma_start(out=xw_all[:], in_=x_words[0].rearrange("p n t -> p (n t)").bitcast(I32))
-        nc.sync.dma_start(out=w_raw[0][:].bitcast(I32), in_=w2_words[0].bitcast(I32))
         nc.sync.dma_start(out=w_raw[1][:].bitcast(I32), in_=w1_words[0].bitcast(I32))
-        load_scale_rows(nc, ws_raw[0], w2_scales)
+        nc.sync.dma_start(out=xw_all[:], in_=x_words[0].rearrange("p n t -> p (n t)").bitcast(I32))
         load_scale_rows(nc, ws_raw[1], w1_scales)
+        nc.sync.dma_start(out=w_raw[0][:].bitcast(I32), in_=w2_words[0].bitcast(I32))
+        load_scale_rows(nc, ws_raw[0], w2_scales)
         nc.sync.dma_start(sel_t[:], sel)
         nc.sync.dma_start(out=ctx_t[:], in_=ctx2.rearrange("(p t) v -> p t v", t=PACK))
         nc.sync.dma_start(out=unit_t[:], in_=unit.rearrange("(p t) o -> p (t o)", t=PACK))
@@ -72,8 +75,8 @@ def tile_picked_ymodsk_nxt_p_kernel(
 
         def deal(i):
             nc.vector.tensor_copy(
-                out=w_deal[i][:].rearrange("p (t m b) -> p t m b", t=PACK, b=2),
-                in_=w_raw[i][:].rearrange("p (m t b) -> p t m b", t=PACK, b=2),
+                out=w_deal[i][:].bitcast(U16).rearrange("p (t m) -> p t m", t=PACK),
+                in_=w_raw[i][:].bitcast(U16).rearrange("p (m t) -> p t m", t=PACK),
             )
             nc.vector.tensor_copy(
                 out=ws_deal[i][:].rearrange("p (t m) -> p t m", t=PACK),
@@ -84,8 +87,8 @@ def tile_picked_ymodsk_nxt_p_kernel(
         xw = keep.tile([P, S], U32, name="xw", align_bytes=64)
         nc.vector.tensor_copy(xs[:], xs_all[:].indirect(offs_t[:]))
         nc.vector.tensor_copy(xw[:], xw_all[:].bitcast(U32).indirect(offs_t[:]))
-        deal(0)
         deal(1)
+        deal(0)
 
         scaled = keep.tile([P, PACK, S], F32, name="scaled")
         fetched = [keep.tile([P, PACK, CHUNK], F32, name="fetched%d" % h) for h in range(CHUNKS)]
@@ -200,15 +203,15 @@ def tile_picked_ymodsk_nxt_p_kernel(
                 nc.scalar.copy(res[:], acc[:])
             nc.sync.dma_start(out=out[:, CHUNK * h : CHUNK * (h + 1)], in_=res[:])
 
-        er(0)
-        ey(0,"v")
+        ey(0,"s")
         ey(1,"s")
         ey(2,"s")
+        er(0)
         add(0)
         add(1)
-        ey(3,"s")
-        sg(0)
         add(2)
+        sg(0)
+        ey(3,"v")
         sg(1)
         er(1)
         gmul(0)
@@ -232,7 +235,7 @@ def tile_picked_ymodsk_nxt_p_kernel(
         scale(3,"v")
         scale(2,"v")
         fetch(0,0,"v")
-        fetch(1,0,"s")
+        fetch(1,0,"v")
         fetch(3,0,"s")
         fetch(2,0,"s")
         fetch(0,1,"v")

@@ -40,7 +40,7 @@ def tile_picked_ymodsk_nxt_p_kernel(
         offs_t = keep.tile([P, S // 16], U16, name="offs_t")
         sel_t = keep.tile([P, V // 16], U16, name="sel_t")
         nxt_t = keep.tile([P, S // 16], U16, name="nxt_t")
-        xw_all = keep.tile([P, T], I32, name="xw_all", align_bytes=64)
+        xw_all = keep.tile([P, T], I32, name="xw_all", tag="x_table", align_bytes=64)
         xs_all = keep.tile([P, T], U8, name="xs_all", align_bytes=64)
         w_raw = [keep.tile([P, 2 * H], U8, name="w_raw%d" % i, align_bytes=64) for i in range(2)]
         ws_raw = [keep.tile([P, H], U8, name="ws_raw%d" % i, align_bytes=64) for i in range(2)]
@@ -50,27 +50,27 @@ def tile_picked_ymodsk_nxt_p_kernel(
         unit_t = keep.tile([P, PACK], F32, name="unit_t")
 
         warm = keep.tile([P, 16], F32, name="warm")
+        nc.vector.memset(xs_all[:].bitcast(I32), 0)
         nc.vector.memset(warm[:, 0:1], 0.0)
         nc.scalar.activation(warm[:, 8:9], warm[:, 0:1], ACT.Sigmoid)
-        nc.gpsimd.memset(xs_all[:].bitcast(I32), 0)
         for plane in (ws_raw[1], ws_raw[0], w3s):
-            nc.gpsimd.memset(plane[:].bitcast(I32), 0)
+            nc.vector.memset(plane[:].bitcast(I32), 0)
 
         nc.sync.dma_start(offs_t[:], offs)
         load_scale_rows(nc, xs_all, x_scales)
-        nc.sync.dma_start(out=w_raw[1][:].bitcast(I32), in_=w1_words[0].bitcast(I32))
         nc.sync.dma_start(out=xw_all[:], in_=x_words[0].rearrange("p n t -> p (n t)").bitcast(I32))
-        load_scale_rows(nc, ws_raw[1], w1_scales)
-        nc.sync.dma_start(out=w_raw[0][:].bitcast(I32), in_=w2_words[0].bitcast(I32))
-        load_scale_rows(nc, ws_raw[0], w2_scales)
+        nc.sync.dma_start(out=w_raw[1][:].bitcast(I32), in_=w1_words[0].bitcast(I32))
         nc.sync.dma_start(sel_t[:], sel)
-        nc.sync.dma_start(out=ctx_t[:], in_=ctx2.rearrange("(p t) v -> p t v", t=PACK))
+        load_scale_rows(nc, ws_raw[1], w1_scales)
+        load_scale_rows(nc, ws_raw[0], w2_scales)
+        nc.gpsimd.dma_start(out=w_raw[0][:].bitcast(I32), in_=w2_words[0].bitcast(I32))
+        nc.gpsimd.dma_start(out=w3w[:].bitcast(I32), in_=w3_words[0].bitcast(I32))
+        nc.gpsimd.dma_start(out=ctx_t[:], in_=ctx2.rearrange("(p t) v -> p t v", t=PACK))
         nc.sync.dma_start(out=unit_t[:], in_=unit.rearrange("(p t) o -> p (t o)", t=PACK))
         nc.sync.dma_start(nxt_t[:], nxt)
-        nc.sync.dma_start(out=w3w[:].bitcast(I32), in_=w3_words[0].bitcast(I32))
         load_scale_rows(nc, w3s, w3_scales)
 
-        w_deal = [keep.tile([P, 2 * H], U8, name="w_deal%d" % i, align_bytes=64) for i in range(2)]
+
         ws_deal = [keep.tile([P, H], U8, name="ws_deal%d" % i, align_bytes=64) for i in range(2)]
 
         def deal(i):
@@ -87,6 +87,10 @@ def tile_picked_ymodsk_nxt_p_kernel(
         xw = keep.tile([P, S], U32, name="xw", align_bytes=64)
         nc.vector.tensor_copy(xs[:], xs_all[:].indirect(offs_t[:]))
         nc.vector.tensor_copy(xw[:], xw_all[:].bitcast(U32).indirect(offs_t[:]))
+        w_deal = [
+            keep.tile([P, 2 * H], U8, name="w2_deal", tag="x_table", align_bytes=64),
+            keep.tile([P, 2 * H], U8, name="w1_deal", align_bytes=64),
+        ]
         deal(1)
         deal(0)
 

@@ -40,10 +40,10 @@ def tile_picked_ymodsk_nxt_p_kernel(
         offs_t = keep.tile([P, S // 16], U16, name="offs_t")
         sel_t = keep.tile([P, V // 16], U16, name="sel_t")
         nxt_t = keep.tile([P, S // 16], U16, name="nxt_t")
-        xw_all = keep.tile([P, T], I32, name="xw_all", tag="x_table", align_bytes=64)
+        xw_all = keep.tile([P, T], I32, name="xw_all", align_bytes=64)
         xs_all = keep.tile([P, T], U8, name="xs_all", align_bytes=64)
         w_raw = [keep.tile([P, 2 * H], U8, name="w_raw%d" % i, align_bytes=64) for i in range(2)]
-        ws_raw = [keep.tile([P, H], U8, name="ws_raw%d" % i, align_bytes=64) for i in range(2)]
+        ws_raw = [keep.tile([P, H], U8, name="ws_raw%d" % i, tag="ws_raw%d" % i, align_bytes=64) for i in range(2)]
         w3w = keep.tile([P, 2 * N], U8, name="w3w", align_bytes=64)
         w3s = keep.tile([P, N], U8, name="w3s", align_bytes=64)
         ctx_t = keep.tile([P, PACK, V], F32, name="ctx_t")
@@ -58,8 +58,8 @@ def tile_picked_ymodsk_nxt_p_kernel(
 
         nc.sync.dma_start(offs_t[:], offs)
         load_scale_rows(nc, xs_all, x_scales)
-        nc.sync.dma_start(out=xw_all[:], in_=x_words[0].rearrange("p n t -> p (n t)").bitcast(I32))
         nc.sync.dma_start(out=w_raw[1][:].bitcast(I32), in_=w1_words[0].bitcast(I32))
+        nc.sync.dma_start(out=xw_all[:], in_=x_words[0].rearrange("p n t -> p (n t)").bitcast(I32))
         nc.sync.dma_start(sel_t[:], sel)
         load_scale_rows(nc, ws_raw[1], w1_scales)
         load_scale_rows(nc, ws_raw[0], w2_scales)
@@ -87,11 +87,9 @@ def tile_picked_ymodsk_nxt_p_kernel(
         xw = keep.tile([P, S], U32, name="xw", align_bytes=64)
         nc.vector.tensor_copy(xs[:], xs_all[:].indirect(offs_t[:]))
         nc.vector.tensor_copy(xw[:], xw_all[:].bitcast(U32).indirect(offs_t[:]))
-        w_deal = [
-            keep.tile([P, 2 * H], U8, name="w2_deal", tag="x_table", align_bytes=64),
-            keep.tile([P, 2 * H], U8, name="w1_deal", align_bytes=64),
-        ]
+        w_deal = {1: keep.tile([P, 2 * H], U8, name="w1_deal", align_bytes=64)}
         deal(1)
+        w_deal.setdefault(0, keep.tile([P, 2 * H], U8, name="w2_deal", tag="ws_raw1", align_bytes=64))
         deal(0)
 
         scaled = keep.tile([P, PACK, S], F32, name="scaled")
@@ -210,24 +208,24 @@ def tile_picked_ymodsk_nxt_p_kernel(
         ey(0,"s")
         ey(1,"s")
         ey(2,"s")
-        er(0)
         add(0)
         add(1)
         add(2)
+        er(0)
         sg(0)
         ey(3,"v")
-        sg(1)
         er(1)
+        sg(1)
         gmul(0)
         add(3)
-        sg(2)
         er(2)
+        sg(2)
         upd(0,u)
         gmul(1)
-        sg(3)
         er(3)
-        upd(1,u)
+        sg(3)
         gmul(2)
+        upd(1,u)
         upd(2,u)
         gmul(3)
         put(0)
@@ -238,27 +236,27 @@ def tile_picked_ymodsk_nxt_p_kernel(
         scale(1,"v")
         scale(3,"v")
         scale(2,"v")
-        fetch(0,0,"v")
-        fetch(1,0,"v")
-        fetch(3,0,"s")
-        fetch(2,0,"s")
-        fetch(0,1,"v")
+        fetch(0,0,"s")
+        fetch(1,0,"s")
+        fetch(3,0,"v")
+        fetch(2,0,"v")
+        diff4(0)
+        fetch(0,1,"s")
         fetch(1,1,"s")
-        fetch(3,1,"s")
-        fetch(2,1,"s")
-        fetch(0,2,"v")
+        fetch(3,1,"v")
+        fetch(2,1,"v")
+        diff4(1)
+        finish(0,"s")
+        fetch(0,2,"s")
         fetch(1,2,"s")
         fetch(3,2,"s")
         fetch(2,2,"s")
-        fetch(0,3,"v")
+        diff4(2)
+        finish(1,"s")
+        fetch(0,3,"s")
         fetch(1,3,"s")
         fetch(3,3,"s")
         fetch(2,3,"s")
-        diff4(0)
-        diff4(1)
-        finish(0,"s")
-        diff4(2)
-        finish(1,"s")
         diff4(3)
         finish(2,"s")
-        finish(3,"s")
+        finish(3,"v")

@@ -16,15 +16,40 @@ ACT = mybir.ActivationFunctionType
 ALU = mybir.AluOpType
 
 P = 128
-T, S, V, H, N = 1024, 512, 256, 512, 128
+T = 1024
+S = 512
+V = 256
+H = 512
+N = 128
 PACK = 4
-CHUNKS = 4
-CHUNK = S // CHUNKS
+LIST_COL = 16
+HALF = S // 2
+CHUNK = 128
+CHUNKS = S // CHUNK
+RUN = 4
+
+LAST = PACK - 1
+EARLY_TILES = 2
+VECTOR_FETCH_TILES = (2, 3)
+VECTOR_FETCH_CHUNKS = 2
 
 
-def load_scale_rows(nc, plane, rows):
+def load_scale_rows(nc, scale_tile, rows):
     for q in range(4):
-        nc.sync.dma_start(out=plane[32 * q : 32 * q + 4, :].bitcast(I32), in_=rows[0, 4 * q : 4 * q + 4, :].bitcast(I32))
+        nc.sync.dma_start(
+            out=scale_tile[32 * q : 32 * q + 4, :].bitcast(I32), in_=rows[0, 4 * q : 4 * q + 4, :].bitcast(I32)
+        )
+
+
+def deal_columns(nc, words_out, scales_out, words_in, scales_in):
+    nc.vector.tensor_copy(
+        out=words_out[:].bitcast(U16).rearrange("p (t m) -> p t m", t=PACK),
+        in_=words_in[:].bitcast(U16).rearrange("p (m t) -> p t m", t=PACK),
+    )
+    nc.vector.tensor_copy(
+        out=scales_out[:].rearrange("p (t m) -> p t m", t=PACK),
+        in_=scales_in[:].rearrange("p (m t) -> p t m", t=PACK),
+    )
 
 
 def tile_picked_ymodsk_nxt_p_kernel(
@@ -33,230 +58,159 @@ def tile_picked_ymodsk_nxt_p_kernel(
     nc = tc.nc
     with ExitStack() as stack:
         keep = stack.enter_context(tc.tile_pool(name="keep", bufs=1))
-        ring = stack.enter_context(tc.tile_pool(name="ring", bufs=4))
-        psum = stack.enter_context(tc.psum_pool(name="psum", bufs=3))
-        psum_out = stack.enter_context(tc.psum_pool(name="psum_out", bufs=2))
+        each = stack.enter_context(tc.tile_pool(name="each", bufs=PACK))
+        psum = stack.enter_context(tc.psum_pool(name="psum", bufs=8))
 
-        offs_t = keep.tile([P, S // 16], U16, name="offs_t")
-        sel_t = keep.tile([P, V // 16], U16, name="sel_t")
-        nxt_t = keep.tile([P, S // 16], U16, name="nxt_t")
-        xw_all = keep.tile([P, T], I32, name="xw_all", align_bytes=64)
-        xs_all = keep.tile([P, T], U8, name="xs_all", align_bytes=64)
-        w_raw = [keep.tile([P, 2 * H], U8, name="w_raw%d" % i, align_bytes=64) for i in range(2)]
-        ws_raw = [keep.tile([P, H], U8, name="ws_raw%d" % i, tag="ws_raw%d" % i, align_bytes=64) for i in range(2)]
-        w3w = keep.tile([P, 2 * N], U8, name="w3w", align_bytes=64)
-        w3s = keep.tile([P, N], U8, name="w3s", align_bytes=64)
-        ctx_t = keep.tile([P, PACK, V], F32, name="ctx_t")
-        unit_t = keep.tile([P, PACK], F32, name="unit_t")
+        offs_list = keep.tile([P, S // LIST_COL], U16, name="offs_list")
+        sel_list = keep.tile([P, V // LIST_COL], U16, name="sel_list")
+        nxt_list = keep.tile([P, S // LIST_COL], U16, name="nxt_list")
+        table_words = keep.tile([P, T], I32, name="table_words", tag="table_words", align_bytes=64)
+        table_scales = keep.tile([P, T], U8, name="table_scales", align_bytes=64)
+        w1_raw_words = keep.tile([P, 2 * H], U8, name="w1_raw_words", align_bytes=64)
+        w2_raw_words = keep.tile([P, 2 * H], U8, name="w2_raw_words", align_bytes=64)
+        w1_raw_scales = keep.tile([P, H], U8, name="w1_raw_scales", tag="w1_raw_scales", align_bytes=64)
+        w2_raw_scales = keep.tile([P, H], U8, name="w2_raw_scales", align_bytes=64)
+        w3_codes = keep.tile([P, 2 * N], U8, name="w3_codes", align_bytes=64)
+        w3_scale = keep.tile([P, N], U8, name="w3_scale", align_bytes=64)
+        context = keep.tile([P, PACK, V], F32, name="context")
+        units = keep.tile([P, PACK], F32, name="units")
 
+        nc.vector.memset(table_scales[:].bitcast(I32), 0)
         warm = keep.tile([P, 16], F32, name="warm")
-        nc.vector.memset(xs_all[:].bitcast(I32), 0)
         nc.vector.memset(warm[:, 0:1], 0.0)
         nc.scalar.activation(warm[:, 8:9], warm[:, 0:1], ACT.Sigmoid)
-        for plane in (ws_raw[1], ws_raw[0], w3s):
-            nc.vector.memset(plane[:].bitcast(I32), 0)
+        for scale_tile in (w1_raw_scales, w2_raw_scales, w3_scale):
+            nc.vector.memset(scale_tile[:].bitcast(I32), 0)
 
-        nc.sync.dma_start(offs_t[:], offs)
-        load_scale_rows(nc, xs_all, x_scales)
-        nc.sync.dma_start(out=w_raw[1][:].bitcast(I32), in_=w1_words[0].bitcast(I32))
-        nc.sync.dma_start(out=xw_all[:], in_=x_words[0].rearrange("p n t -> p (n t)").bitcast(I32))
-        nc.sync.dma_start(sel_t[:], sel)
-        load_scale_rows(nc, ws_raw[1], w1_scales)
-        load_scale_rows(nc, ws_raw[0], w2_scales)
-        nc.gpsimd.dma_start(out=w_raw[0][:].bitcast(I32), in_=w2_words[0].bitcast(I32))
-        nc.gpsimd.dma_start(out=w3w[:].bitcast(I32), in_=w3_words[0].bitcast(I32))
-        nc.gpsimd.dma_start(out=ctx_t[:], in_=ctx2.rearrange("(p t) v -> p t v", t=PACK))
-        nc.sync.dma_start(out=unit_t[:], in_=unit.rearrange("(p t) o -> p (t o)", t=PACK))
-        nc.sync.dma_start(nxt_t[:], nxt)
-        load_scale_rows(nc, w3s, w3_scales)
+        nc.sync.dma_start(offs_list[:], offs)
+        load_scale_rows(nc, table_scales, x_scales)
+        nc.sync.dma_start(out=w1_raw_words[:].bitcast(I32), in_=w1_words[0].bitcast(I32))
+        nc.sync.dma_start(out=table_words[:], in_=x_words[0].rearrange("p n r -> p (n r)").bitcast(I32))
+        nc.sync.dma_start(sel_list[:], sel)
+        load_scale_rows(nc, w1_raw_scales, w1_scales)
+        load_scale_rows(nc, w2_raw_scales, w2_scales)
+        nc.gpsimd.dma_start(out=w2_raw_words[:].bitcast(I32), in_=w2_words[0].bitcast(I32))
+        nc.gpsimd.dma_start(out=w3_codes[:].bitcast(I32), in_=w3_words[0].bitcast(I32))
+        nc.gpsimd.dma_start(out=context[:], in_=ctx2.rearrange("(p t) v -> p t v", t=PACK))
+        nc.sync.dma_start(out=units[:], in_=unit.rearrange("(p t) o -> p (t o)", t=PACK))
+        nc.sync.dma_start(nxt_list[:], nxt)
+        load_scale_rows(nc, w3_scale, w3_scales)
 
+        x_scale = keep.tile([P, S], U8, name="x_scale", align_bytes=64)
+        w1_codes = keep.tile([P, 2 * H], U8, name="w1_codes", align_bytes=64)
+        w1_scale = keep.tile([P, H], U8, name="w1_scale", align_bytes=64)
+        w2_scale = keep.tile([P, H], U8, name="w2_scale", align_bytes=64)
+        half_cols = HALF // LIST_COL
+        x_first = keep.tile([P, HALF], U32, name="x_first", align_bytes=64)
+        nc.vector.tensor_copy(x_scale[:], table_scales[:].indirect(offs_list[:]))
+        nc.vector.tensor_copy(x_first[:], table_words[:].bitcast(U32).indirect(offs_list[:, 0:half_cols]))
+        deal_columns(nc, w1_codes, w1_scale, w1_raw_words, w1_raw_scales)
+        x_second = keep.tile([P, HALF], U32, name="x_second", tag="w1_raw_scales", align_bytes=64)
+        nc.vector.tensor_copy(x_second[:], table_words[:].bitcast(U32).indirect(offs_list[:, half_cols : 2 * half_cols]))
+        w2_codes = keep.tile([P, 2 * H], U8, name="w2_codes", tag="table_words", align_bytes=64)
+        deal_columns(nc, w2_codes, w2_scale, w2_raw_words, w2_raw_scales)
+        x_codes = (x_first, x_second)
 
-        ws_deal = [keep.tile([P, H], U8, name="ws_deal%d" % i, align_bytes=64) for i in range(2)]
-
-        def deal(i):
-            nc.vector.tensor_copy(
-                out=w_deal[i][:].bitcast(U16).rearrange("p (t m) -> p t m", t=PACK),
-                in_=w_raw[i][:].bitcast(U16).rearrange("p (m t) -> p t m", t=PACK),
-            )
-            nc.vector.tensor_copy(
-                out=ws_deal[i][:].rearrange("p (t m) -> p t m", t=PACK),
-                in_=ws_raw[i][:].rearrange("p (m t) -> p t m", t=PACK),
-            )
-
-        xs = keep.tile([P, S], U8, name="xs", align_bytes=64)
-        xw = keep.tile([P, S], U32, name="xw", align_bytes=64)
-        nc.vector.tensor_copy(xs[:], xs_all[:].indirect(offs_t[:]))
-        nc.vector.tensor_copy(xw[:], xw_all[:].bitcast(U32).indirect(offs_t[:]))
-        w_deal = {1: keep.tile([P, 2 * H], U8, name="w1_deal", align_bytes=64)}
-        deal(1)
-        w_deal.setdefault(0, keep.tile([P, 2 * H], U8, name="w2_deal", tag="ws_raw1", align_bytes=64))
-        deal(0)
-
-        scaled = keep.tile([P, PACK, S], F32, name="scaled")
-        fetched = [keep.tile([P, PACK, CHUNK], F32, name="fetched%d" % h) for h in range(CHUNKS)]
-
-        def product(i, t, tag):
-            acc = psum.tile([P, S], F32, name=tag)
-            nc.tensor.matmul_mx(
-                out=acc[:],
-                lhsT=w_deal[i][:, 2 * P * t : 2 * P * (t + 1)].bitcast(FP4X4),
-                lhsT_scale=ws_deal[i][:, P * t : P * (t + 1)],
-                rhs=xw[:].bitcast(FP8X4),
-                rhs_scale=xs[:],
-                start=True,
-                stop=True,
-            )
+        def product(codes, scale, t, halves):
+            acc = psum.tile([P, HALF * len(halves)], F32, name="acc")
+            for place, half in enumerate(halves):
+                nc.tensor.matmul_mx(
+                    out=acc[:, HALF * place : HALF * (place + 1)],
+                    lhsT=codes[:, 2 * P * t : 2 * P * (t + 1)].bitcast(FP4X4),
+                    lhsT_scale=scale[:, P * t : P * (t + 1)],
+                    rhs=x_codes[half][:].bitcast(FP8X4),
+                    rhs_scale=x_scale[:, HALF * half : HALF * (half + 1)],
+                    start=True,
+                    stop=True,
+                )
             return acc
 
-        accs, merged, gate, u, su, rw, g = {}, {}, {}, {}, {}, {}, {}
-        for t in range(PACK):
-            merged[t] = ring.tile([P, S], F32, name="merged")
-            gate[t] = ring.tile([P, S], F32, name="gate")
-            u[t] = ring.tile([P, V], F32, name="u")
-            su[t] = ring.tile([P, V], F32, name="su")
-            rw[t] = ring.tile([P, V], F32, name="rw")
-            g[t] = ring.tile([P, V], F32, name="g")
+        tiles = range(PACK)
+        merged = [each.tile([P, S], F32, name="merged") for t in tiles]
+        gate = [each.tile([P, S], F32, name="gate") for t in tiles]
+        pre = [each.tile([P, V], F32, name="pre") for t in tiles]
+        pre_sigmoid = [each.tile([P, V], F32, name="pre_sigmoid") for t in tiles]
+        both = [each.tile([P, V], F32, name="both") for t in tiles]
+        update = [each.tile([P, V], F32, name="update") for t in range(LAST)]
 
-        def ey(t, eng="s"):
-            acc = product(1, t, "y")
-            if eng == "v":
-                nc.vector.tensor_copy(merged[t][:], acc[:])
-            else:
-                nc.scalar.copy(merged[t][:], acc[:])
+        def add_context(t):
+            nc.vector.tensor_tensor(pre[t][:], merged[t][:].indirect(sel_list[:]), context[:, t, :], ALU.add)
 
-        def er(t):
-            acc = product(0, t, "yr")
-            nc.scalar.activation(gate[t][:], acc[:], ACT.Sigmoid)
+        def make_gate(t):
+            nc.scalar.activation(gate[t][:], product(w2_codes, w2_scale, t, (0, 1))[:], ACT.Sigmoid)
 
-        def add(t):
-            nc.vector.tensor_tensor(u[t][:], merged[t][:].indirect(sel_t[:]), ctx_t[:, t, :], ALU.add)
+        for half in range(2):
+            for t in range(EARLY_TILES):
+                acc = product(w1_codes, w1_scale, t, (half,))
+                nc.scalar.copy(merged[t][:, HALF * half : HALF * (half + 1)], acc[:])
+        for t in range(EARLY_TILES, LAST):
+            nc.scalar.copy(merged[t][:], product(w1_codes, w1_scale, t, (0, 1))[:])
+        for t in range(LAST):
+            add_context(t)
+        make_gate(0)
+        nc.vector.tensor_copy(merged[LAST][:], product(w1_codes, w1_scale, LAST, (0, 1))[:])
+        add_context(LAST)
 
-        def sg(t):
-            nc.scalar.activation(su[t][:], u[t][:], ACT.Sigmoid)
+        for t in tiles:
+            nc.scalar.activation(pre_sigmoid[t][:], pre[t][:], ACT.Sigmoid)
+            if t < LAST:
+                make_gate(t + 1)
+        for t in tiles:
+            nc.vector.tensor_tensor(both[t][:], gate[t][:].indirect(sel_list[:]), pre_sigmoid[t][:], ALU.mult)
+            if t < LAST:
+                nc.vector.tensor_tensor(update[t][:], both[t][:], pre[t][:], ALU.mult)
 
-        def gg(t):
-            nc.scalar.activation(rw[t][:], gate[t][:].indirect(sel_t[:]), ACT.Copy)
+        for t in range(LAST):
+            nc.scalar.activation(merged[t][:].indirect(sel_list[:]), update[t][:], ACT.Copy)
+        nc.vector.tensor_tensor(merged[LAST][:].indirect(sel_list[:]), both[LAST][:], pre[LAST][:], ALU.mult)
 
-        def mul(t):
-            nc.vector.tensor_tensor(g[t][:], u[t][:], su[t][:], ALU.mult)
+        scatter_order = (0, 1, LAST, 2)
+        scaled = keep.tile([P, PACK, S], F32, name="scaled")
+        for t in scatter_order:
+            nc.vector.tensor_scalar(scaled[:, t, :], merged[t][:], units[:, t : t + 1], None, ALU.mult)
 
-        def gmul(t):
-            nc.vector.tensor_tensor(g[t][:], gate[t][:].indirect(sel_t[:]), su[t][:], ALU.mult)
-
-        def scat(t, other):
-            nc.vector.tensor_tensor(merged[t][:].indirect(sel_t[:]), g[t][:], other[t][:], ALU.mult)
-
-        def scat_s(t, other):
-            upd = ring.tile([P, V], F32, name="upd")
-            nc.vector.tensor_tensor(upd[:], g[t][:], other[t][:], ALU.mult)
-            nc.scalar.activation(merged[t][:].indirect(sel_t[:]), upd[:], ACT.Copy)
-
-        upds = {}
-
-        def upd(t, other):
-            upds[t] = ring.tile([P, V], F32, name="upd")
-            nc.vector.tensor_tensor(upds[t][:], g[t][:], other[t][:], ALU.mult)
-
-        def put(t):
-            nc.scalar.activation(merged[t][:].indirect(sel_t[:]), upds[t][:], ACT.Copy)
-
-        def scale(t, eng):
-            if eng == "v":
-                nc.vector.tensor_scalar(scaled[:, t, :], merged[t][:], unit_t[:, t : t + 1], None, ALU.mult)
-            else:
-                nc.scalar.activation(scaled[:, t, :], merged[t][:], ACT.Copy, scale=unit_t[:, t : t + 1])
-
-        def fetch(t, h, eng):
-            cols = CHUNK // 16
-            src = scaled[:, t, :].indirect(nxt_t[:, cols * h : cols * (h + 1)])
-            if eng == "v":
-                nc.vector.tensor_copy(fetched[h][:, t, :], src)
-            else:
-                nc.scalar.activation(fetched[h][:, t, :], src, ACT.Copy)
-
-        hid = [ring.tile([P, CHUNK * PACK], BF16, name="hid", align_bytes=64) for h in range(CHUNKS)]
-
-        def diff4(h):
+        def quantise_chunk_input(c):
+            chunk_cols = CHUNK // LIST_COL
+            fetched = each.tile([P, PACK, CHUNK], F32, name="fetched")
+            for t in scatter_order:
+                neighbours = scaled[:, t, :].indirect(nxt_list[:, chunk_cols * c : chunk_cols * (c + 1)])
+                if t in VECTOR_FETCH_TILES and c < VECTOR_FETCH_CHUNKS:
+                    nc.vector.tensor_copy(fetched[:, t, :], neighbours)
+                else:
+                    nc.scalar.activation(fetched[:, t, :], neighbours, ACT.Copy)
+            hid = each.tile([P, CHUNK * PACK], BF16, name="hid", align_bytes=64)
             nc.vector.tensor_tensor(
-                hid[h][:].rearrange("p (c i t) -> p c t i", i=4, t=PACK),
-                scaled[:, :, CHUNK * h : CHUNK * (h + 1)].rearrange("p t (c i) -> p c t i", i=4),
-                fetched[h][:].rearrange("p t (c i) -> p c t i", i=4),
+                hid[:].rearrange("p (g j t) -> p g t j", j=RUN, t=PACK),
+                scaled[:, :, CHUNK * c : CHUNK * (c + 1)].rearrange("p t (g j) -> p g t j", j=RUN),
+                fetched[:].rearrange("p t (g j) -> p g t j", j=RUN),
                 ALU.subtract,
             )
+            return hid
 
-        def finish(h, eng):
-            hw = ring.tile([P, CHUNK], U32, name="hw", align_bytes=64)
-            hs = ring.tile([P, CHUNK], U8, name="hs", align_bytes=64)
-            nc.vector.quantize_mx(out=hw[:].bitcast(FP8X4), scales=hs[:], in_=hid[h][:])
-            acc = psum_out.tile([P, CHUNK], F32, name="acc")
+        def last_product(c, hid):
+            hid_codes = each.tile([P, CHUNK], U32, name="hid_codes", align_bytes=64)
+            hid_scale = each.tile([P, CHUNK], U8, name="hid_scale", align_bytes=64)
+            nc.vector.quantize_mx(out=hid_codes[:].bitcast(FP8X4), scales=hid_scale[:], in_=hid[:])
+            acc = psum.tile([P, CHUNK], F32, name="acc")
             nc.tensor.matmul_mx(
                 out=acc[:],
-                lhsT=w3w[:].bitcast(FP4X4),
-                lhsT_scale=w3s[:],
-                rhs=hw[:].bitcast(FP8X4),
-                rhs_scale=hs[:],
+                lhsT=w3_codes[:].bitcast(FP4X4),
+                lhsT_scale=w3_scale[:],
+                rhs=hid_codes[:].bitcast(FP8X4),
+                rhs_scale=hid_scale[:],
                 start=True,
                 stop=True,
             )
-            res = ring.tile([P, CHUNK], F32, name="res")
-            if eng == "v":
-                nc.vector.tensor_copy(res[:], acc[:])
+            result = each.tile([P, CHUNK], F32, name="result")
+            if c == CHUNKS - 1:
+                nc.vector.tensor_copy(result[:], acc[:])
             else:
-                nc.scalar.copy(res[:], acc[:])
-            nc.sync.dma_start(out=out[:, CHUNK * h : CHUNK * (h + 1)], in_=res[:])
+                nc.scalar.copy(result[:], acc[:])
+            nc.sync.dma_start(out=out[:, CHUNK * c : CHUNK * (c + 1)], in_=result[:])
 
-        ey(0,"s")
-        ey(1,"s")
-        ey(2,"s")
-        add(0)
-        add(1)
-        add(2)
-        er(0)
-        sg(0)
-        ey(3,"v")
-        er(1)
-        sg(1)
-        gmul(0)
-        add(3)
-        er(2)
-        sg(2)
-        upd(0,u)
-        gmul(1)
-        er(3)
-        sg(3)
-        gmul(2)
-        upd(1,u)
-        upd(2,u)
-        gmul(3)
-        put(0)
-        put(1)
-        scale(0,"v")
-        scat(3,u)
-        put(2)
-        scale(1,"v")
-        scale(3,"v")
-        scale(2,"v")
-        fetch(0,0,"s")
-        fetch(1,0,"s")
-        fetch(3,0,"v")
-        fetch(2,0,"v")
-        diff4(0)
-        fetch(0,1,"s")
-        fetch(1,1,"s")
-        fetch(3,1,"v")
-        fetch(2,1,"v")
-        diff4(1)
-        finish(0,"s")
-        fetch(0,2,"s")
-        fetch(1,2,"s")
-        fetch(3,2,"s")
-        fetch(2,2,"s")
-        diff4(2)
-        finish(1,"s")
-        fetch(0,3,"s")
-        fetch(1,3,"s")
-        fetch(3,3,"s")
-        fetch(2,3,"s")
-        diff4(3)
-        finish(2,"s")
-        finish(3,"v")
+        hids = []
+        for c in range(CHUNKS):
+            hids.append(quantise_chunk_input(c))
+            if c > 0:
+                last_product(c - 1, hids[c - 1])
+        last_product(CHUNKS - 1, hids[CHUNKS - 1])

from contextlib import ExitStack

import concourse.mybir as mybir

FLOPS = 603979776

F32 = mybir.dt.float32
BF16 = mybir.dt.bfloat16
I32 = mybir.dt.int32
U32 = mybir.dt.uint32
U16 = mybir.dt.uint16
U8 = mybir.dt.uint8
FP8X4 = mybir.dt.float8_e4m3fn_x4
FP4X4 = mybir.dt.float4_e2m1fn_x4
ACT = mybir.ActivationFunctionType
ALU = mybir.AluOpType

P = 128
T = 1024
S = 512
V = 256
H = 512
N = 128
PACK = 4
LIST_COL = 16
HALF = S // 2
CHUNK = 128
CHUNKS = S // CHUNK
RUN = 4

LAST = PACK - 1
EARLY_TILES = 2
VECTOR_FETCH_TILES = (2, 3)
VECTOR_FETCH_CHUNKS = 2


def load_scale_rows(nc, scale_tile, rows):
    for q in range(4):
        nc.sync.dma_start(
            out=scale_tile[32 * q : 32 * q + 4, :].bitcast(I32), in_=rows[0, 4 * q : 4 * q + 4, :].bitcast(I32)
        )


def deal_columns(nc, words_out, scales_out, words_in, scales_in):
    nc.vector.tensor_copy(
        out=words_out[:].bitcast(U16).rearrange("p (t m) -> p t m", t=PACK),
        in_=words_in[:].bitcast(U16).rearrange("p (m t) -> p t m", t=PACK),
    )
    nc.vector.tensor_copy(
        out=scales_out[:].rearrange("p (t m) -> p t m", t=PACK),
        in_=scales_in[:].rearrange("p (m t) -> p t m", t=PACK),
    )


def tile_picked_ymodsk_nxt_p_kernel(
    tc, x_words, x_scales, w1_words, w1_scales, w2_words, w2_scales, ctx2, unit, w3_words, w3_scales, offs, sel, nxt, out
):
    nc = tc.nc
    with ExitStack() as stack:
        keep = stack.enter_context(tc.tile_pool(name="keep", bufs=1))
        each = stack.enter_context(tc.tile_pool(name="each", bufs=PACK))
        psum = stack.enter_context(tc.psum_pool(name="psum", bufs=8))

        offs_list = keep.tile([P, S // LIST_COL], U16, name="offs_list")
        sel_list = keep.tile([P, V // LIST_COL], U16, name="sel_list")
        nxt_list = keep.tile([P, S // LIST_COL], U16, name="nxt_list")
        table_words = keep.tile([P, T], I32, name="table_words", tag="table_words", align_bytes=64)
        table_scales = keep.tile([P, T], U8, name="table_scales", align_bytes=64)
        w1_raw_words = keep.tile([P, 2 * H], U8, name="w1_raw_words", align_bytes=64)
        w2_raw_words = keep.tile([P, 2 * H], U8, name="w2_raw_words", align_bytes=64)
        w1_raw_scales = keep.tile([P, H], U8, name="w1_raw_scales", tag="w1_raw_scales", align_bytes=64)
        w2_raw_scales = keep.tile([P, H], U8, name="w2_raw_scales", align_bytes=64)
        w3_codes = keep.tile([P, 2 * N], U8, name="w3_codes", align_bytes=64)
        w3_scale = keep.tile([P, N], U8, name="w3_scale", align_bytes=64)
        context = keep.tile([P, PACK, V], F32, name="context")
        units = keep.tile([P, PACK], F32, name="units")

        nc.vector.memset(table_scales[:].bitcast(I32), 0)
        warm = keep.tile([P, 16], F32, name="warm")
        nc.vector.memset(warm[:, 0:1], 0.0)
        nc.scalar.activation(warm[:, 8:9], warm[:, 0:1], ACT.Sigmoid)
        for scale_tile in (w1_raw_scales, w2_raw_scales, w3_scale):
            nc.vector.memset(scale_tile[:].bitcast(I32), 0)

        nc.sync.dma_start(offs_list[:], offs)
        load_scale_rows(nc, table_scales, x_scales)
        nc.sync.dma_start(out=w1_raw_words[:].bitcast(I32), in_=w1_words[0].bitcast(I32))
        nc.sync.dma_start(out=table_words[:], in_=x_words[0].rearrange("p n r -> p (n r)").bitcast(I32))
        nc.sync.dma_start(sel_list[:], sel)
        load_scale_rows(nc, w1_raw_scales, w1_scales)
        load_scale_rows(nc, w2_raw_scales, w2_scales)
        nc.gpsimd.dma_start(out=w2_raw_words[:].bitcast(I32), in_=w2_words[0].bitcast(I32))
        nc.gpsimd.dma_start(out=w3_codes[:].bitcast(I32), in_=w3_words[0].bitcast(I32))
        nc.gpsimd.dma_start(out=context[:], in_=ctx2.rearrange("(p t) v -> p t v", t=PACK))
        nc.sync.dma_start(out=units[:], in_=unit.rearrange("(p t) o -> p (t o)", t=PACK))
        nc.sync.dma_start(nxt_list[:], nxt)
        load_scale_rows(nc, w3_scale, w3_scales)

        x_scale = keep.tile([P, S], U8, name="x_scale", align_bytes=64)
        w1_codes = keep.tile([P, 2 * H], U8, name="w1_codes", align_bytes=64)
        w1_scale = keep.tile([P, H], U8, name="w1_scale", align_bytes=64)
        w2_scale = keep.tile([P, H], U8, name="w2_scale", align_bytes=64)
        half_cols = HALF // LIST_COL
        x_first = keep.tile([P, HALF], U32, name="x_first", align_bytes=64)
        nc.vector.tensor_copy(x_scale[:], table_scales[:].indirect(offs_list[:]))
        nc.vector.tensor_copy(x_first[:], table_words[:].bitcast(U32).indirect(offs_list[:, 0:half_cols]))
        deal_columns(nc, w1_codes, w1_scale, w1_raw_words, w1_raw_scales)
        x_second = keep.tile([P, HALF], U32, name="x_second", tag="w1_raw_scales", align_bytes=64)
        nc.vector.tensor_copy(x_second[:], table_words[:].bitcast(U32).indirect(offs_list[:, half_cols : 2 * half_cols]))
        w2_codes = keep.tile([P, 2 * H], U8, name="w2_codes", tag="table_words", align_bytes=64)
        deal_columns(nc, w2_codes, w2_scale, w2_raw_words, w2_raw_scales)
        x_codes = (x_first, x_second)

        def product(codes, scale, t, halves):
            acc = psum.tile([P, HALF * len(halves)], F32, name="acc")
            for place, half in enumerate(halves):
                nc.tensor.matmul_mx(
                    out=acc[:, HALF * place : HALF * (place + 1)],
                    lhsT=codes[:, 2 * P * t : 2 * P * (t + 1)].bitcast(FP4X4),
                    lhsT_scale=scale[:, P * t : P * (t + 1)],
                    rhs=x_codes[half][:].bitcast(FP8X4),
                    rhs_scale=x_scale[:, HALF * half : HALF * (half + 1)],
                    start=True,
                    stop=True,
                )
            return acc

        tiles = range(PACK)
        merged = [each.tile([P, S], F32, name="merged") for t in tiles]
        gate = [each.tile([P, S], F32, name="gate") for t in tiles]
        pre = [each.tile([P, V], F32, name="pre") for t in tiles]
        pre_sigmoid = [each.tile([P, V], F32, name="pre_sigmoid") for t in tiles]
        both = [each.tile([P, V], F32, name="both") for t in tiles]
        update = [each.tile([P, V], F32, name="update") for t in range(LAST)]

        def add_context(t):
            nc.vector.tensor_tensor(pre[t][:], merged[t][:].indirect(sel_list[:]), context[:, t, :], ALU.add)

        def make_gate(t):
            nc.scalar.activation(gate[t][:], product(w2_codes, w2_scale, t, (0, 1))[:], ACT.Sigmoid)

        for half in range(2):
            for t in range(EARLY_TILES):
                acc = product(w1_codes, w1_scale, t, (half,))
                nc.scalar.copy(merged[t][:, HALF * half : HALF * (half + 1)], acc[:])
        for t in range(EARLY_TILES, LAST):
            nc.scalar.copy(merged[t][:], product(w1_codes, w1_scale, t, (0, 1))[:])
        for t in range(LAST):
            add_context(t)
        make_gate(0)
        nc.vector.tensor_copy(merged[LAST][:], product(w1_codes, w1_scale, LAST, (0, 1))[:])
        add_context(LAST)

        for t in tiles:
            nc.scalar.activation(pre_sigmoid[t][:], pre[t][:], ACT.Sigmoid)
            if t < LAST:
                make_gate(t + 1)
        for t in tiles:
            nc.vector.tensor_tensor(both[t][:], gate[t][:].indirect(sel_list[:]), pre_sigmoid[t][:], ALU.mult)
            if t < LAST:
                nc.vector.tensor_tensor(update[t][:], both[t][:], pre[t][:], ALU.mult)

        for t in range(LAST):
            nc.scalar.activation(merged[t][:].indirect(sel_list[:]), update[t][:], ACT.Copy)
        nc.vector.tensor_tensor(merged[LAST][:].indirect(sel_list[:]), both[LAST][:], pre[LAST][:], ALU.mult)

        scatter_order = (0, 1, LAST, 2)
        scaled = keep.tile([P, PACK, S], F32, name="scaled")
        for t in scatter_order:
            nc.vector.tensor_scalar(scaled[:, t, :], merged[t][:], units[:, t : t + 1], None, ALU.mult)

        def quantise_chunk_input(c):
            chunk_cols = CHUNK // LIST_COL
            fetched = each.tile([P, PACK, CHUNK], F32, name="fetched")
            for t in scatter_order:
                neighbours = scaled[:, t, :].indirect(nxt_list[:, chunk_cols * c : chunk_cols * (c + 1)])
                if t in VECTOR_FETCH_TILES and c < VECTOR_FETCH_CHUNKS:
                    nc.vector.tensor_copy(fetched[:, t, :], neighbours)
                else:
                    nc.scalar.activation(fetched[:, t, :], neighbours, ACT.Copy)
            hid = each.tile([P, CHUNK * PACK], BF16, name="hid", align_bytes=64)
            nc.vector.tensor_tensor(
                hid[:].rearrange("p (g j t) -> p g t j", j=RUN, t=PACK),
                scaled[:, :, CHUNK * c : CHUNK * (c + 1)].rearrange("p t (g j) -> p g t j", j=RUN),
                fetched[:].rearrange("p t (g j) -> p g t j", j=RUN),
                ALU.subtract,
            )
            return hid

        def last_product(c, hid):
            hid_codes = each.tile([P, CHUNK], U32, name="hid_codes", align_bytes=64)
            hid_scale = each.tile([P, CHUNK], U8, name="hid_scale", align_bytes=64)
            nc.vector.quantize_mx(out=hid_codes[:].bitcast(FP8X4), scales=hid_scale[:], in_=hid[:])
            acc = psum.tile([P, CHUNK], F32, name="acc")
            nc.tensor.matmul_mx(
                out=acc[:],
                lhsT=w3_codes[:].bitcast(FP4X4),
                lhsT_scale=w3_scale[:],
                rhs=hid_codes[:].bitcast(FP8X4),
                rhs_scale=hid_scale[:],
                start=True,
                stop=True,
            )
            result = each.tile([P, CHUNK], F32, name="result")
            if c == CHUNKS - 1:
                nc.vector.tensor_copy(result[:], acc[:])
            else:
                nc.scalar.copy(result[:], acc[:])
            nc.sync.dma_start(out=out[:, CHUNK * c : CHUNK * (c + 1)], in_=result[:])

        hids = []
        for c in range(CHUNKS):
            hids.append(quantise_chunk_input(c))
            if c > 0:
                last_product(c - 1, hids[c - 1])
        last_product(CHUNKS - 1, hids[CHUNKS - 1])
